import numpy as np
import ml_dtypes


def mxq(x, axis, fmt="e4m3"):
    dtype, down = {"e4m3": (ml_dtypes.float8_e4m3fn, 7), "e5m2": (ml_dtypes.float8_e5m2, 14)}[fmt]
    v = np.moveaxis(np.asarray(x, np.float32).astype(ml_dtypes.bfloat16).astype(np.float64), axis, -1)
    blocks = v.reshape(v.shape[:-1] + (-1, 32))
    amax = np.abs(blocks).max(-1, keepdims=True)
    byte = np.maximum(np.where(amax > 0, np.frexp(amax)[1] - 1 + 127, 0) - down, 1)
    scale = np.exp2(byte - 127.0)
    codes = (blocks / scale).astype(np.float32).astype(dtype).astype(np.float64)
    return np.moveaxis((codes * scale).reshape(v.shape), -1, axis)


WIDE = False


def mx_kscale(k):
    if not WIDE:
        return np.ones(k)
    levels = np.array([10, -10, 5, -5, 0])
    if k % 512:
        return np.exp2(np.random.permutation(np.resize(levels, k // 32))).repeat(32)
    a = np.empty((k // 512, 16))
    for p in range(k // 512):
        a[p, :8] = np.random.permutation(np.resize(levels, 8))
        for g in range(8):
            far = levels[np.abs(levels - a[p, g]) >= 10]
            a[p, g + 8] = far[np.random.randint(len(far))]
    return np.exp2(a.ravel()).repeat(32)


def f64(x):
    return np.asarray(x).astype(np.float64)


def striped(idx):
    return np.tile(idx.reshape(-1, 16).T, (8, 1)).astype(np.uint16)


def unstriped(offs):
    return offs[:16].T.reshape(-1).astype(np.int64)


E2M1 = np.array([0.0, 0.5, 1.0, 1.5, 2.0, 3.0, 4.0, 6.0, -0.0, -0.5, -1.0, -1.5, -2.0, -3.0, -4.0, -6.0])


def pack_weight(w, fmt):
    k, n = w.shape
    w = f64(np.asarray(w, np.float32).astype(ml_dtypes.bfloat16)).reshape(k // 32, 32, n)
    amax = np.abs(w).max(1)
    if fmt == "e4m3":
        byte = np.frexp(amax)[1] - 1 + 127 - 7
    else:
        mant, ex = np.frexp(amax / 6.0)
        byte = np.where(mant > 0.5, ex, ex - 1) + 127
    byte = np.clip(np.where(amax > 0, byte, 1), 1, 254)
    scaled = (w * np.exp2(127.0 - byte)[:, None, :]).reshape(k, n).astype(np.float32)
    by_word = np.ascontiguousarray(scaled.reshape(k // 512, 128, 4, n).transpose(0, 1, 3, 2))
    if fmt == "e4m3":
        words = by_word.astype(ml_dtypes.float8_e4m3fn).view(np.uint8)
    else:
        c = by_word.astype(ml_dtypes.float4_e2m1fn).view(np.uint8) & 0xF
        words = (c[..., 0::2] | (c[..., 1::2] << 4)).reshape(k // 512, 128, 2 * n)
    return np.ascontiguousarray(words), np.ascontiguousarray(byte.astype(np.uint8).reshape(k // 512, 16, n))


def unpack_weight(words, scales, fmt):
    g, _, n = scales.shape
    words = np.ascontiguousarray(words).reshape(g, 128, n, -1)
    if fmt == "e4m3":
        vals = words.view(ml_dtypes.float8_e4m3fn).astype(np.float64)
    else:
        nib = np.empty((g, 128, n, 4), np.uint8)
        nib[..., 0::2] = words & 0xF
        nib[..., 1::2] = words >> 4
        vals = E2M1[nib]
    vals = vals * np.repeat(np.exp2(scales.astype(np.float64) - 127.0), 8, axis=1)[..., None]
    return vals.transpose(0, 1, 3, 2).reshape(g * 512, n)


def silu(v):
    return v / (1.0 + np.exp(-np.maximum(v, -700.0)))


G, K, M, T, S = 2, 512, 1024, 1024, 256


def setup_inputs():
    n = np.random.standard_normal
    s = mx_kscale(K)[:, None]
    p_w4 = pack_weight(n((K, M)) / np.sqrt(K) / s, "e2m1")
    p_w8 = pack_weight(n((K, M)) / np.sqrt(K) / s, "e4m3")
    return {
        "xT": (n((K, T)) * s).astype(np.float32),
        "c": (n((K, S)) * s).astype(np.float32),
        "w4_words": p_w4[0],
        "w4_scales": p_w4[1],
        "w8_words": p_w8[0],
        "w8_scales": p_w8[1],
        "b": (0.3 * n(1024)).astype(np.float32),
        "offs": striped(np.concatenate([np.random.permutation(T)[:S] for _ in range(G)])),
    }


def reference(xT, c, w4_words, w4_scales, w8_words, w8_scales, b, offs):
    idx = unstriped(offs).reshape(G, S)
    d_ = [mxq(f64(xT)[:, idx[g]] - f64(c), 0, "e4m3") for g in range(G)]
    c_ = mxq(f64(c), 0, "e4m3")
    w4_ = unpack_weight(w4_words, w4_scales, "e2m1")
    w8_ = unpack_weight(w8_words, w8_scales, "e4m3")
    y = np.max([(d.T @ w4_) for d in d_], axis=0) + (c_.T @ w8_)
    return silu(y + f64(b)[None, :])

@@ -1,0 +1,169 @@
+from contextlib import ExitStack
+
+import concourse.mybir as mybir
+from concourse.masks import make_identity
+
+G, K, M, T, S = 2, 512, 1024, 1024, 256
+FLOPS = 2 * K * M * S * (G + 1)
+
+F32 = mybir.dt.float32
+BF16 = mybir.dt.bfloat16
+I32 = mybir.dt.int32
+U32 = mybir.dt.uint32
+U16 = mybir.dt.uint16
+U8 = mybir.dt.uint8
+FP8X4 = mybir.dt.float8_e4m3fn_x4
+FP4X4 = mybir.dt.float4_e2m1fn_x4
+ALU = mybir.AluOpType
+ACT = mybir.ActivationFunctionType
+
+P = 128
+PACK = 4
+NT = 512
+
+
+def tile_list_edge_tm_silu_kernel(tc, xT, c, w4_words, w4_scales, w8_words, w8_scales, b, offs, out):
+    nc = tc.nc
+    with ExitStack() as ctx:
+        keep = ctx.enter_context(tc.tile_pool(name="keep", bufs=1))
+        ring = ctx.enter_context(tc.tile_pool(name="ring", bufs=4))
+        psum = ctx.enter_context(tc.psum_pool(name="psum", bufs=8))
+
+        lists = keep.tile([P, G * S // 16], U16, name="lists")
+        nc.sync.dma_start(lists[:], offs)
+
+        s4 = keep.tile([P, M], U8, name="s4", align_bytes=64)
+        s8 = keep.tile([P, M], U8, name="s8", align_bytes=64)
+        nc.vector.memset(s8[:].bitcast(I32), 0)
+        nc.vector.memset(s4[:].bitcast(I32), 0)
+        warm = keep.tile([P, 1], F32, name="warm")
+        nc.vector.memset(warm[:], 0.0)
+        warm_out = keep.tile([P, 1], F32, name="warm_out")
+        nc.scalar.activation(warm_out[:], warm[:], ACT.Silu)
+
+        b_cols = keep.tile([P, 8], F32, name="b_cols")
+        nc.gpsimd.dma_start(b_cols[:], b.rearrange("(p t) -> p t", t=8))
+        ident = keep.tile([P, P], F32, name="ident")
+        make_identity(nc, ident[:])
+        for q in range(4):
+            nc.gpsimd.dma_start(s8[32 * q : 32 * q + 4, :].bitcast(I32), w8_scales[0, 4 * q : 4 * q + 4, :].bitcast(I32))
+
+        x_rows = xT.rearrange("(p i) t -> p i t", i=PACK)
+        c_rows = c.rearrange("(p i) j -> p i j", i=PACK)
+        x = [keep.tile([P, T], F32, name="x%d" % i) for i in range(PACK)]
+        own = keep.tile([P, PACK, S], F32, name="own")
+        nc.sync.dma_start(x[0][:], x_rows[:, 0, :])
+        nc.sync.dma_start(own[:, 0, :], c_rows[:, 0, :])
+        nc.sync.dma_start(x[1][:], x_rows[:, 1, :])
+        nc.sync.dma_start(own[:, 1:, :], c_rows[:, 1:, :])
+        nc.sync.dma_start(x[2][:], x_rows[:, 2, :])
+        nc.sync.dma_start(x[3][:], x_rows[:, 3, :])
+        for q in range(4):
+            nc.sync.dma_start(s4[32 * q : 32 * q + 4, :].bitcast(I32), w4_scales[0, 4 * q : 4 * q + 4, :].bitcast(I32))
+        w8_rows = w8_words[0].rearrange("p n t -> p (n t)")
+        w8 = [keep.tile([P, NT], U32, name="w8_%d" % h, align_bytes=64) for h in range(2)]
+        for h in range(2):
+            nc.sync.dma_start(w8[h][:].bitcast(I32), w8_rows[:, h * 4 * NT : (h + 1) * 4 * NT].bitcast(I32))
+        w4 = keep.tile([P, 2 * M], U8, name="w4", align_bytes=64)
+        nc.sync.dma_start(w4[:].bitcast(I32), w4_words[0].bitcast(I32))
+
+        bias = keep.tile([P, P, 8], F32, name="bias")
+        for h in range(2):
+            spread = psum.tile([P, 4, P], F32, name="bank", tag="bank")
+            for t in range(4):
+                nc.tensor.transpose(spread[:, t, :], b_cols[:, 4 * h + t : 4 * h + t + 1].to_broadcast([P, P]), ident[:])
+            nc.scalar.copy(bias[:, :, 4 * h : 4 * h + 4], spread[:].rearrange("p t n -> p n t"))
+        bias_row = bias[:].rearrange("p n t -> p (n t)")
+
+        diff = [keep.tile([P, 2, G, S], F32, name="diff%d" % u) for u in range(2)]
+        woven = [keep.tile([P, G, P, PACK], BF16, name="woven%d" % jh, align_bytes=64) for jh in range(2)]
+        d_codes = [keep.tile([P, G * P], U32, name="dc%d" % jh, align_bytes=64) for jh in range(2)]
+        d_scales = [keep.tile([P, G * P], U8, name="ds%d" % jh, align_bytes=64) for jh in range(2)]
+
+        def gather(i, g, j0, j1):
+            nc.vector.tensor_tensor(
+                diff[i // 2][:, i % 2, g, j0:j1],
+                x[i][:].indirect(lists[:, (g * S + j0) // 16 : (g * S + j1) // 16]),
+                own[:, i, j0:j1],
+                ALU.subtract,
+            )
+
+        def weave(copy, u, jh, g0, g1):
+            copy(
+                woven[jh][:, g0:g1, :, 2 * u : 2 * u + 2],
+                diff[u][:, :, g0:g1, jh * P : (jh + 1) * P].rearrange("p i g j -> p g j i"),
+            )
+
+        def quantize(jh):
+            nc.vector.quantize_mx(
+                out=d_codes[jh][:].bitcast(FP8X4), scales=d_scales[jh][:], in_=woven[jh][:].rearrange("p g j i -> p (g j i)")
+            )
+
+        for i in range(2):
+            for g in range(G):
+                gather(i, g, 0, S)
+        own_woven = keep.tile([P, S, PACK], BF16, name="own_woven", align_bytes=64)
+        nc.scalar.copy(own_woven[:], own[:].rearrange("p i j -> p j i"))
+        for jh in range(2):
+            weave(nc.scalar.copy, 0, jh, 0, G)
+        for g in range(G):
+            gather(2, g, 0, S)
+        c_codes = keep.tile([P, S], U32, name="c_codes", align_bytes=64)
+        c_scales = keep.tile([P, S], U8, name="c_scales", align_bytes=64)
+        nc.vector.quantize_mx(out=c_codes[:].bitcast(FP8X4), scales=c_scales[:], in_=own_woven[:].rearrange("p j i -> p (j i)"))
+        for jh in range(2):
+            for g in range(G):
+                gather(3, g, jh * P, (jh + 1) * P)
+        weave(nc.scalar.copy, 1, 0, 0, 1)
+        weave(nc.scalar.copy, 1, 0, 1, 2)
+        weave(nc.scalar.copy, 1, 1, 0, 1)
+        quantize(0)
+        weave(nc.vector.tensor_copy, 1, 1, 1, 2)
+        quantize(1)
+
+        def node_part(jh, nh):
+            z = psum.tile([P, NT], F32, name="bank", tag="bank")
+            nc.tensor.matmul_mx(
+                out=z[:],
+                lhsT=c_codes[:, jh * P : (jh + 1) * P].bitcast(FP8X4),
+                lhsT_scale=c_scales[:, jh * P : (jh + 1) * P],
+                rhs=w8[nh][:].bitcast(FP8X4),
+                rhs_scale=s8[:, nh * NT : (nh + 1) * NT],
+                start=True,
+                stop=True,
+            )
+            return z
+
+        def edge_part(jh, nh, g):
+            y = psum.tile([P, NT], F32, name="bank", tag="bank")
+            nc.tensor.matmul_mx(
+                out=y[:],
+                lhsT=d_codes[jh][:, g * P : (g + 1) * P].bitcast(FP8X4),
+                lhsT_scale=d_scales[jh][:, g * P : (g + 1) * P],
+                rhs=w4[:, nh * 2 * NT : (nh + 1) * 2 * NT].bitcast(FP4X4),
+                rhs_scale=s4[:, nh * NT : (nh + 1) * NT],
+                start=True,
+                stop=True,
+            )
+            return y
+
+        order = [(0, 0), (0, 1), (1, 0), (1, 1)]
+        z = {}
+        for jh, nh in [(0, 0), (1, 0), (0, 1), (1, 1)]:
+            z[jh, nh] = node_part(jh, nh)
+        for n, (jh, nh) in enumerate(order):
+            cols = slice(nh * NT, (nh + 1) * NT)
+            y0 = edge_part(jh, nh, 0)
+            y1 = edge_part(jh, nh, 1)
+            biased = ring.tile([P, NT], F32, name="biased")
+            nc.vector.tensor_tensor(biased[:], z[jh, nh][:], bias_row[:, cols], ALU.add)
+            first = ring.tile([P, NT], F32, name="first")
+            nc.scalar.copy(first[:], y0[:])
+            larger = ring.tile([P, NT], F32, name="larger")
+            nc.vector.tensor_tensor(larger[:], y1[:], first[:], ALU.max)
+            total = ring.tile([P, NT], F32, name="total")
+            adder = nc.vector if n == 3 else nc.gpsimd
+            adder.tensor_tensor(total[:], larger[:], biased[:], ALU.add)
+            result = ring.tile([P, NT], F32, name="result")
+            nc.scalar.activation(result[:], total[:], ACT.Silu)
+            nc.sync.dma_start(out[jh * P : (jh + 1) * P, cols], result[:])

@@ -27,11 +27,10 @@ def tile_list_edge_tm_silu_kernel(tc, xT, c, w4_words, w4_scales, w8_words, w8_s
     with ExitStack() as ctx:
         keep = ctx.enter_context(tc.tile_pool(name="keep", bufs=1))
         ring = ctx.enter_context(tc.tile_pool(name="ring", bufs=4))
-        psum = ctx.enter_context(tc.psum_pool(name="psum", bufs=8))
+        psum = ctx.enter_context(tc.psum_pool(name="psum", bufs=1))
 
         lists = keep.tile([P, G * S // 16], U16, name="lists")
-        nc.sync.dma_start(lists[:], offs)
-
+        b_cols = keep.tile([P, 8], F32, name="b_cols")
         s4 = keep.tile([P, M], U8, name="s4", align_bytes=64)
         s8 = keep.tile([P, M], U8, name="s8", align_bytes=64)
         nc.vector.memset(s8[:].bitcast(I32), 0)
@@ -40,43 +39,42 @@ def tile_list_edge_tm_silu_kernel(tc, xT, c, w4_words, w4_scales, w8_words, w8_s
         nc.vector.memset(warm[:], 0.0)
         warm_out = keep.tile([P, 1], F32, name="warm_out")
         nc.scalar.activation(warm_out[:], warm[:], ACT.Silu)
-
-        b_cols = keep.tile([P, 8], F32, name="b_cols")
-        nc.gpsimd.dma_start(b_cols[:], b.rearrange("(p t) -> p t", t=8))
         ident = keep.tile([P, P], F32, name="ident")
         make_identity(nc, ident[:])
-        for q in range(4):
-            nc.gpsimd.dma_start(s8[32 * q : 32 * q + 4, :].bitcast(I32), w8_scales[0, 4 * q : 4 * q + 4, :].bitcast(I32))
 
         x_rows = xT.rearrange("(p i) t -> p i t", i=PACK)
         c_rows = c.rearrange("(p i) j -> p i j", i=PACK)
         x = [keep.tile([P, T], F32, name="x%d" % i) for i in range(PACK)]
         own = keep.tile([P, PACK, S], F32, name="own")
-        nc.sync.dma_start(x[0][:], x_rows[:, 0, :])
-        nc.sync.dma_start(own[:, 0, :], c_rows[:, 0, :])
-        nc.sync.dma_start(x[1][:], x_rows[:, 1, :])
-        nc.sync.dma_start(own[:, 1:, :], c_rows[:, 1:, :])
-        nc.sync.dma_start(x[2][:], x_rows[:, 2, :])
-        nc.sync.dma_start(x[3][:], x_rows[:, 3, :])
-        for q in range(4):
-            nc.sync.dma_start(s4[32 * q : 32 * q + 4, :].bitcast(I32), w4_scales[0, 4 * q : 4 * q + 4, :].bitcast(I32))
         w8_rows = w8_words[0].rearrange("p n t -> p (n t)")
         w8 = [keep.tile([P, NT], U32, name="w8_%d" % h, align_bytes=64) for h in range(2)]
-        for h in range(2):
-            nc.sync.dma_start(w8[h][:].bitcast(I32), w8_rows[:, h * 4 * NT : (h + 1) * 4 * NT].bitcast(I32))
         w4 = keep.tile([P, 2 * M], U8, name="w4", align_bytes=64)
+        nc.sync.dma_start(b_cols[:], b.rearrange("(p t) -> p t", t=8))
+        nc.sync.dma_start(x[0][:], x_rows[:, 0, :])
+        nc.sync.dma_start(lists[:], offs)
+        nc.sync.dma_start(own[:, :2, :], c_rows[:, :2, :])
+        nc.sync.dma_start(own[:, 2:, :], c_rows[:, 2:, :])
+        nc.sync.dma_start(x[1][:], x_rows[:, 1, :])
+        nc.sync.dma_start(x[2][:], x_rows[:, 2, :])
+        for q in range(4):
+            nc.sync.dma_start(s8[32 * q : 32 * q + 4, :].bitcast(I32), w8_scales[0, 4 * q : 4 * q + 4, :].bitcast(I32))
+        nc.sync.dma_start(w8[0][:].bitcast(I32), w8_rows[:, : 4 * NT].bitcast(I32))
+        nc.sync.dma_start(x[3][:], x_rows[:, 3, :])
+        nc.sync.dma_start(w8[1][:].bitcast(I32), w8_rows[:, 4 * NT :].bitcast(I32))
         nc.sync.dma_start(w4[:].bitcast(I32), w4_words[0].bitcast(I32))
+        for q in range(4):
+            nc.sync.dma_start(s4[32 * q : 32 * q + 4, :].bitcast(I32), w4_scales[0, 4 * q : 4 * q + 4, :].bitcast(I32))
 
         bias = keep.tile([P, P, 8], F32, name="bias")
         for h in range(2):
-            spread = psum.tile([P, 4, P], F32, name="bank", tag="bank")
+            spread = psum.tile([P, 4, P], F32, name="spread", tag="bank%d" % h)
             for t in range(4):
                 nc.tensor.transpose(spread[:, t, :], b_cols[:, 4 * h + t : 4 * h + t + 1].to_broadcast([P, P]), ident[:])
             nc.scalar.copy(bias[:, :, 4 * h : 4 * h + 4], spread[:].rearrange("p t n -> p n t"))
         bias_row = bias[:].rearrange("p n t -> p (n t)")
 
-        diff = [keep.tile([P, 2, G, S], F32, name="diff%d" % u) for u in range(2)]
-        woven = [keep.tile([P, G, P, PACK], BF16, name="woven%d" % jh, align_bytes=64) for jh in range(2)]
+        diff = [keep.tile([P, 2, G, S], F32, name="diff%d" % u, tag="diff%d" % u, align_bytes=64) for u in range(2)]
+        woven = [keep.tile([P, G, P, PACK], BF16, name="woven%d" % jh, tag="woven%d" % jh, align_bytes=64) for jh in range(2)]
         d_codes = [keep.tile([P, G * P], U32, name="dc%d" % jh, align_bytes=64) for jh in range(2)]
         d_scales = [keep.tile([P, G * P], U8, name="ds%d" % jh, align_bytes=64) for jh in range(2)]
 
@@ -104,25 +102,25 @@ def tile_list_edge_tm_silu_kernel(tc, xT, c, w4_words, w4_scales, w8_words, w8_s
                 gather(i, g, 0, S)
         own_woven = keep.tile([P, S, PACK], BF16, name="own_woven", align_bytes=64)
         nc.scalar.copy(own_woven[:], own[:].rearrange("p i j -> p j i"))
+        c_codes = keep.tile([P, S], U32, name="c_codes", align_bytes=64)
+        c_scales = keep.tile([P, S], U8, name="c_scales", align_bytes=64)
+        nc.vector.quantize_mx(out=c_codes[:].bitcast(FP8X4), scales=c_scales[:], in_=own_woven[:].rearrange("p j i -> p (j i)"))
         for jh in range(2):
             weave(nc.scalar.copy, 0, jh, 0, G)
         for g in range(G):
             gather(2, g, 0, S)
-        c_codes = keep.tile([P, S], U32, name="c_codes", align_bytes=64)
-        c_scales = keep.tile([P, S], U8, name="c_scales", align_bytes=64)
-        nc.vector.quantize_mx(out=c_codes[:].bitcast(FP8X4), scales=c_scales[:], in_=own_woven[:].rearrange("p j i -> p (j i)"))
         for jh in range(2):
             for g in range(G):
                 gather(3, g, jh * P, (jh + 1) * P)
         weave(nc.scalar.copy, 1, 0, 0, 1)
         weave(nc.scalar.copy, 1, 0, 1, 2)
         weave(nc.scalar.copy, 1, 1, 0, 1)
+        weave(nc.scalar.copy, 1, 1, 1, 2)
         quantize(0)
-        weave(nc.vector.tensor_copy, 1, 1, 1, 2)
         quantize(1)
 
         def node_part(jh, nh):
-            z = psum.tile([P, NT], F32, name="bank", tag="bank")
+            z = psum.tile([P, NT], F32, name="node", tag="bank%d" % (4 + 2 * jh + nh))
             nc.tensor.matmul_mx(
                 out=z[:],
                 lhsT=c_codes[:, jh * P : (jh + 1) * P].bitcast(FP8X4),
@@ -134,8 +132,8 @@ def tile_list_edge_tm_silu_kernel(tc, xT, c, w4_words, w4_scales, w8_words, w8_s
             )
             return z
 
-        def edge_part(jh, nh, g):
-            y = psum.tile([P, NT], F32, name="bank", tag="bank")
+        def edge_part(jh, nh, g, bank):
+            y = psum.tile([P, NT], F32, name="edge", tag="bank%d" % bank)
             nc.tensor.matmul_mx(
                 out=y[:],
                 lhsT=d_codes[jh][:, g * P : (g + 1) * P].bitcast(FP8X4),
@@ -151,19 +149,40 @@ def tile_list_edge_tm_silu_kernel(tc, xT, c, w4_words, w4_scales, w8_words, w8_s
         z = {}
         for jh, nh in [(0, 0), (1, 0), (0, 1), (1, 1)]:
             z[jh, nh] = node_part(jh, nh)
+        biased, larger, total = [], [], []
+
+        def finish(n, engine, n0, n1):
+            engine.tensor_tensor(total[n][:, n0:n1], larger[n][:, n0:n1], biased[n][:, n0:n1], ALU.add)
+
+        def emit(n, n0, n1):
+            jh, nh = order[n]
+            result = ring.tile([P, n1 - n0], F32, name="result", tag="result")
+            nc.scalar.activation(result[:], total[n][:, n0:n1], ACT.Silu)
+            nc.sync.dma_start(out[jh * P : (jh + 1) * P, nh * NT + n0 : nh * NT + n1], result[:])
+
+        def add_bias(n, tag):
+            jh, nh = order[n]
+            biased.append(keep.tile([P, NT], F32, name="biased%d" % n, tag=tag, align_bytes=64))
+            nc.vector.tensor_tensor(biased[n][:], z[jh, nh][:], bias_row[:, nh * NT : (nh + 1) * NT], ALU.add)
+
+        add_bias(0, "woven0")
+        add_bias(1, "diff1")
         for n, (jh, nh) in enumerate(order):
-            cols = slice(nh * NT, (nh + 1) * NT)
-            y0 = edge_part(jh, nh, 0)
-            y1 = edge_part(jh, nh, 1)
-            biased = ring.tile([P, NT], F32, name="biased")
-            nc.vector.tensor_tensor(biased[:], z[jh, nh][:], bias_row[:, cols], ALU.add)
+            y0 = edge_part(jh, nh, 0, (0, 2, 4, 0)[n])
+            y1 = edge_part(jh, nh, 1, (1, 3, 5, 1)[n])
             first = ring.tile([P, NT], F32, name="first")
             nc.scalar.copy(first[:], y0[:])
-            larger = ring.tile([P, NT], F32, name="larger")
-            nc.vector.tensor_tensor(larger[:], y1[:], first[:], ALU.max)
-            total = ring.tile([P, NT], F32, name="total")
-            adder = nc.vector if n == 3 else nc.gpsimd
-            adder.tensor_tensor(total[:], larger[:], biased[:], ALU.add)
-            result = ring.tile([P, NT], F32, name="result")
-            nc.scalar.activation(result[:], total[:], ACT.Silu)
-            nc.sync.dma_start(out[jh * P : (jh + 1) * P, cols], result[:])
+            larger.append(keep.tile([P, NT], F32, name="larger%d" % n, tag="larger%d" % n, align_bytes=64))
+            nc.vector.tensor_tensor(larger[n][:], y1[:], first[:], ALU.max)
+            total.append(ring.tile([P, NT], F32, name="total"))
+        for n in range(2):
+            finish(n, nc.gpsimd, 0, NT)
+            emit(n, 0, NT)
+        add_bias(2, "woven0")
+        add_bias(3, "larger0")
+        finish(2, nc.vector, 0, NT)
+        finish(3, nc.vector, 0, NT // 2)
+        finish(3, nc.vector, NT // 2, NT)
+        emit(2, 0, NT)
+        emit(3, 0, NT // 2)
+        emit(3, NT // 2, NT)

@@ -53,8 +53,8 @@ def tile_list_edge_tm_silu_kernel(tc, xT, c, w4_words, w4_scales, w8_words, w8_s
         nc.sync.dma_start(x[0][:], x_rows[:, 0, :])
         nc.sync.dma_start(lists[:], offs)
         nc.sync.dma_start(own[:, :2, :], c_rows[:, :2, :])
-        nc.sync.dma_start(own[:, 2:, :], c_rows[:, 2:, :])
         nc.sync.dma_start(x[1][:], x_rows[:, 1, :])
+        nc.sync.dma_start(own[:, 2:, :], c_rows[:, 2:, :])
         nc.sync.dma_start(x[2][:], x_rows[:, 2, :])
         for q in range(4):
             nc.sync.dma_start(s8[32 * q : 32 * q + 4, :].bitcast(I32), w8_scales[0, 4 * q : 4 * q + 4, :].bitcast(I32))
@@ -156,7 +156,7 @@ def tile_list_edge_tm_silu_kernel(tc, xT, c, w4_words, w4_scales, w8_words, w8_s
 
         def emit(n, n0, n1):
             jh, nh = order[n]
-            result = ring.tile([P, n1 - n0], F32, name="result", tag="result")
+            result = keep.tile([P, n1 - n0], F32, name="result%d_%d" % (n, n0))
             nc.scalar.activation(result[:], total[n][:, n0:n1], ACT.Silu)
             nc.sync.dma_start(out[jh * P : (jh + 1) * P, nh * NT + n0 : nh * NT + n1], result[:])
 
@@ -170,7 +170,7 @@ def tile_list_edge_tm_silu_kernel(tc, xT, c, w4_words, w4_scales, w8_words, w8_s
         for n, (jh, nh) in enumerate(order):
             y0 = edge_part(jh, nh, 0, (0, 2, 4, 0)[n])
             y1 = edge_part(jh, nh, 1, (1, 3, 5, 1)[n])
-            first = ring.tile([P, NT], F32, name="first")
+            first = keep.tile([P, NT], F32, name="first%d" % n, tag="first%d" % n, align_bytes=64)
             nc.scalar.copy(first[:], y0[:])
             larger.append(keep.tile([P, NT], F32, name="larger%d" % n, tag="larger%d" % n, align_bytes=64))
             nc.vector.tensor_tensor(larger[n][:], y1[:], first[:], ALU.max)
@@ -178,8 +178,8 @@ def tile_list_edge_tm_silu_kernel(tc, xT, c, w4_words, w4_scales, w8_words, w8_s
         for n in range(2):
             finish(n, nc.gpsimd, 0, NT)
             emit(n, 0, NT)
-        add_bias(2, "woven0")
-        add_bias(3, "larger0")
+        add_bias(2, "first0")
+        add_bias(3, "first1")
         finish(2, nc.vector, 0, NT)
         finish(3, nc.vector, 0, NT // 2)
         finish(3, nc.vector, NT // 2, NT)

from contextlib import ExitStack

import concourse.mybir as mybir
from concourse.masks import make_identity

G, K, M, T, S = 2, 512, 1024, 1024, 256
FLOPS = 2 * K * M * S * (G + 1)

F32 = mybir.dt.float32
BF16 = mybir.dt.bfloat16
I32 = mybir.dt.int32
U32 = mybir.dt.uint32
U16 = mybir.dt.uint16
U8 = mybir.dt.uint8
FP8X4 = mybir.dt.float8_e4m3fn_x4
FP4X4 = mybir.dt.float4_e2m1fn_x4
ALU = mybir.AluOpType
ACT = mybir.ActivationFunctionType

P = 128
PACK = 4
NT = 512


def tile_list_edge_tm_silu_kernel(tc, xT, c, w4_words, w4_scales, w8_words, w8_scales, b, offs, out):
    nc = tc.nc
    with ExitStack() as ctx:
        keep = ctx.enter_context(tc.tile_pool(name="keep", bufs=1))
        ring = ctx.enter_context(tc.tile_pool(name="ring", bufs=4))
        psum = ctx.enter_context(tc.psum_pool(name="psum", bufs=1))

        lists = keep.tile([P, G * S // 16], U16, name="lists")
        b_cols = keep.tile([P, 8], F32, name="b_cols")
        s4 = keep.tile([P, M], U8, name="s4", align_bytes=64)
        s8 = keep.tile([P, M], U8, name="s8", align_bytes=64)
        nc.vector.memset(s8[:].bitcast(I32), 0)
        nc.vector.memset(s4[:].bitcast(I32), 0)
        warm = keep.tile([P, 1], F32, name="warm")
        nc.vector.memset(warm[:], 0.0)
        warm_out = keep.tile([P, 1], F32, name="warm_out")
        nc.scalar.activation(warm_out[:], warm[:], ACT.Silu)
        ident = keep.tile([P, P], F32, name="ident")
        make_identity(nc, ident[:])

        x_rows = xT.rearrange("(p i) t -> p i t", i=PACK)
        c_rows = c.rearrange("(p i) j -> p i j", i=PACK)
        x = [keep.tile([P, T], F32, name="x%d" % i) for i in range(PACK)]
        own = keep.tile([P, PACK, S], F32, name="own")
        w8_rows = w8_words[0].rearrange("p n t -> p (n t)")
        w8 = [keep.tile([P, NT], U32, name="w8_%d" % h, align_bytes=64) for h in range(2)]
        w4 = keep.tile([P, 2 * M], U8, name="w4", align_bytes=64)
        nc.sync.dma_start(b_cols[:], b.rearrange("(p t) -> p t", t=8))
        nc.sync.dma_start(x[0][:], x_rows[:, 0, :])
        nc.sync.dma_start(lists[:], offs)
        nc.sync.dma_start(own[:, :2, :], c_rows[:, :2, :])
        nc.sync.dma_start(x[1][:], x_rows[:, 1, :])
        nc.sync.dma_start(own[:, 2:, :], c_rows[:, 2:, :])
        nc.sync.dma_start(x[2][:], x_rows[:, 2, :])
        for q in range(4):
            nc.sync.dma_start(s8[32 * q : 32 * q + 4, :].bitcast(I32), w8_scales[0, 4 * q : 4 * q + 4, :].bitcast(I32))
        nc.sync.dma_start(w8[0][:].bitcast(I32), w8_rows[:, : 4 * NT].bitcast(I32))
        nc.sync.dma_start(x[3][:], x_rows[:, 3, :])
        nc.sync.dma_start(w8[1][:].bitcast(I32), w8_rows[:, 4 * NT :].bitcast(I32))
        nc.sync.dma_start(w4[:].bitcast(I32), w4_words[0].bitcast(I32))
        for q in range(4):
            nc.sync.dma_start(s4[32 * q : 32 * q + 4, :].bitcast(I32), w4_scales[0, 4 * q : 4 * q + 4, :].bitcast(I32))

        bias = keep.tile([P, P, 8], F32, name="bias")
        for h in range(2):
            spread = psum.tile([P, 4, P], F32, name="spread", tag="bank%d" % h)
            for t in range(4):
                nc.tensor.transpose(spread[:, t, :], b_cols[:, 4 * h + t : 4 * h + t + 1].to_broadcast([P, P]), ident[:])
            nc.scalar.copy(bias[:, :, 4 * h : 4 * h + 4], spread[:].rearrange("p t n -> p n t"))
        bias_row = bias[:].rearrange("p n t -> p (n t)")

        diff = [keep.tile([P, 2, G, S], F32, name="diff%d" % u, tag="diff%d" % u, align_bytes=64) for u in range(2)]
        woven = [keep.tile([P, G, P, PACK], BF16, name="woven%d" % jh, tag="woven%d" % jh, align_bytes=64) for jh in range(2)]
        d_codes = [keep.tile([P, G * P], U32, name="dc%d" % jh, align_bytes=64) for jh in range(2)]
        d_scales = [keep.tile([P, G * P], U8, name="ds%d" % jh, align_bytes=64) for jh in range(2)]

        def gather(i, g, j0, j1):
            nc.vector.tensor_tensor(
                diff[i // 2][:, i % 2, g, j0:j1],
                x[i][:].indirect(lists[:, (g * S + j0) // 16 : (g * S + j1) // 16]),
                own[:, i, j0:j1],
                ALU.subtract,
            )

        def weave(copy, u, jh, g0, g1):
            copy(
                woven[jh][:, g0:g1, :, 2 * u : 2 * u + 2],
                diff[u][:, :, g0:g1, jh * P : (jh + 1) * P].rearrange("p i g j -> p g j i"),
            )

        def quantize(jh):
            nc.vector.quantize_mx(
                out=d_codes[jh][:].bitcast(FP8X4), scales=d_scales[jh][:], in_=woven[jh][:].rearrange("p g j i -> p (g j i)")
            )

        for i in range(2):
            for g in range(G):
                gather(i, g, 0, S)
        own_woven = keep.tile([P, S, PACK], BF16, name="own_woven", align_bytes=64)
        nc.scalar.copy(own_woven[:], own[:].rearrange("p i j -> p j i"))
        c_codes = keep.tile([P, S], U32, name="c_codes", align_bytes=64)
        c_scales = keep.tile([P, S], U8, name="c_scales", align_bytes=64)
        nc.vector.quantize_mx(out=c_codes[:].bitcast(FP8X4), scales=c_scales[:], in_=own_woven[:].rearrange("p j i -> p (j i)"))
        for jh in range(2):
            weave(nc.scalar.copy, 0, jh, 0, G)
        for g in range(G):
            gather(2, g, 0, S)
        for jh in range(2):
            for g in range(G):
                gather(3, g, jh * P, (jh + 1) * P)
        weave(nc.scalar.copy, 1, 0, 0, 1)
        weave(nc.scalar.copy, 1, 0, 1, 2)
        weave(nc.scalar.copy, 1, 1, 0, 1)
        weave(nc.scalar.copy, 1, 1, 1, 2)
        quantize(0)
        quantize(1)

        def node_part(jh, nh):
            z = psum.tile([P, NT], F32, name="node", tag="bank%d" % (4 + 2 * jh + nh))
            nc.tensor.matmul_mx(
                out=z[:],
                lhsT=c_codes[:, jh * P : (jh + 1) * P].bitcast(FP8X4),
                lhsT_scale=c_scales[:, jh * P : (jh + 1) * P],
                rhs=w8[nh][:].bitcast(FP8X4),
                rhs_scale=s8[:, nh * NT : (nh + 1) * NT],
                start=True,
                stop=True,
            )
            return z

        def edge_part(jh, nh, g, bank):
            y = psum.tile([P, NT], F32, name="edge", tag="bank%d" % bank)
            nc.tensor.matmul_mx(
                out=y[:],
                lhsT=d_codes[jh][:, g * P : (g + 1) * P].bitcast(FP8X4),
                lhsT_scale=d_scales[jh][:, g * P : (g + 1) * P],
                rhs=w4[:, nh * 2 * NT : (nh + 1) * 2 * NT].bitcast(FP4X4),
                rhs_scale=s4[:, nh * NT : (nh + 1) * NT],
                start=True,
                stop=True,
            )
            return y

        order = [(0, 0), (0, 1), (1, 0), (1, 1)]
        z = {}
        for jh, nh in [(0, 0), (1, 0), (0, 1), (1, 1)]:
            z[jh, nh] = node_part(jh, nh)
        biased, larger, total = [], [], []

        def finish(n, engine, n0, n1):
            engine.tensor_tensor(total[n][:, n0:n1], larger[n][:, n0:n1], biased[n][:, n0:n1], ALU.add)

        def emit(n, n0, n1):
            jh, nh = order[n]
            result = keep.tile([P, n1 - n0], F32, name="result%d_%d" % (n, n0))
            nc.scalar.activation(result[:], total[n][:, n0:n1], ACT.Silu)
            nc.sync.dma_start(out[jh * P : (jh + 1) * P, nh * NT + n0 : nh * NT + n1], result[:])

        def add_bias(n, tag):
            jh, nh = order[n]
            biased.append(keep.tile([P, NT], F32, name="biased%d" % n, tag=tag, align_bytes=64))
            nc.vector.tensor_tensor(biased[n][:], z[jh, nh][:], bias_row[:, nh * NT : (nh + 1) * NT], ALU.add)

        add_bias(0, "woven0")
        add_bias(1, "diff1")
        for n, (jh, nh) in enumerate(order):
            y0 = edge_part(jh, nh, 0, (0, 2, 4, 0)[n])
            y1 = edge_part(jh, nh, 1, (1, 3, 5, 1)[n])
            first = keep.tile([P, NT], F32, name="first%d" % n, tag="first%d" % n, align_bytes=64)
            nc.scalar.copy(first[:], y0[:])
            larger.append(keep.tile([P, NT], F32, name="larger%d" % n, tag="larger%d" % n, align_bytes=64))
            nc.vector.tensor_tensor(larger[n][:], y1[:], first[:], ALU.max)
            total.append(ring.tile([P, NT], F32, name="total"))
        for n in range(2):
            finish(n, nc.gpsimd, 0, NT)
            emit(n, 0, NT)
        add_bias(2, "first0")
        add_bias(3, "first1")
        finish(2, nc.vector, 0, NT)
        finish(3, nc.vector, 0, NT // 2)
        finish(3, nc.vector, NT // 2, NT)
        emit(2, 0, NT)
        emit(3, 0, NT // 2)
        emit(3, NT // 2, NT)
